import numpy as np, ml_dtypes
CORES = [3,0,2,1,6,7,4,5]
N = 8
def setup_inputs(rng):
    return {"x": rng.standard_normal((N, 128, 8192), dtype=np.float32).astype(ml_dtypes.bfloat16)}
def reference(x):
    s = x.max(axis=0)
    b = 8192 // N
    return {"y": np.stack([s[:, r * b:(r + 1) * b] for r in range(N)])}

@@ -1,0 +1,60 @@
+import concourse.bass as bass
+
+N = 8
+B = 8192 // N
+
+SCRATCH = {
+    "xs": ("sbuf", [128, 8192], "bfloat16"),
+    "land": ("sbuf", [128, (N - 1) * B], "bfloat16"),
+    "res": ("sbuf", [128, B], "bfloat16"),
+}
+SEMAPHORES = ["local", "sent", "arrived", "done"]
+
+
+def helper(r):
+    return (r + 1) % N
+
+
+def rank_program(g, core, T, topo):
+    i = T.rank_of(core)
+    if i is None:
+        return
+    mine = (i - 1) % N
+
+    def dst_id(rank):
+        rid, pid, se = topo.addr(T.cores[rank])
+        return bass.DstId(rid=rid, pnc=pid)
+
+    g.dma_start(T.xs[:], T.x[:]).then_inc(T.sem.local, 16)
+    g.wait_ge(T.sem.local, 16)
+
+    transfers = []
+    for r in range(N):
+        h = helper(r)
+        if h == i:
+            continue
+        slot = i if i < h else i - 1
+        transfers.append(bass.RemoteDMATransfer(
+            dst_ids=[dst_id(h)],
+            dma_engine_mask=0b11 << (2 * len(transfers)),
+            remote_sem=T.sem.arrived,
+            src=T.xs[:, r * B:(r + 1) * B],
+            dst=T.land[:, slot * B:(slot + 1) * B],
+        ))
+    g.remote_dma_fused(transfers, local_sem=T.sem.sent)
+
+    g.wait_ge(T.sem.arrived, 2 * (N - 1))
+    srcs = [T.land[:, s * B:(s + 1) * B] for s in range(N - 1)] + [T.xs[:, mine * B:(mine + 1) * B]]
+    g.remote_dma_fused([bass.RemoteDMATransfer(
+        dst_ids=[dst_id(mine)],
+        dma_engine_mask=topo.mask(core, T.cores[mine]),
+        remote_sem=T.sem.done,
+        srcs=srcs,
+        dsts=[T.res[:]],
+        alu_op=2,
+    )], local_sem=T.sem.sent)
+
+    g.wait_ge(T.sem.done, 16)
+    g.dma_start(T.y[:], T.res[:]).then_inc(T.sem.local, 16)
+    g.wait_ge(T.sem.local, 32)
+    g.wait_ge(T.sem.sent, 2 * (N - 1) + 16)

@@ -12,14 +12,14 @@ SEMAPHORES = ["local", "sent", "arrived", "done"]
 
 
 def helper(r):
-    return (r + 1) % N
+    return r ^ 1
 
 
 def rank_program(g, core, T, topo):
     i = T.rank_of(core)
     if i is None:
         return
-    mine = (i - 1) % N
+    mine = i ^ 1
 
     def dst_id(rank):
         rid, pid, se = topo.addr(T.cores[rank])

import concourse.bass as bass

N = 8
B = 8192 // N

SCRATCH = {
    "xs": ("sbuf", [128, 8192], "bfloat16"),
    "land": ("sbuf", [128, (N - 1) * B], "bfloat16"),
    "res": ("sbuf", [128, B], "bfloat16"),
}
SEMAPHORES = ["local", "sent", "arrived", "done"]


def helper(r):
    return r ^ 1


def rank_program(g, core, T, topo):
    i = T.rank_of(core)
    if i is None:
        return
    mine = i ^ 1

    def dst_id(rank):
        rid, pid, se = topo.addr(T.cores[rank])
        return bass.DstId(rid=rid, pnc=pid)

    g.dma_start(T.xs[:], T.x[:]).then_inc(T.sem.local, 16)
    g.wait_ge(T.sem.local, 16)

    transfers = []
    for r in range(N):
        h = helper(r)
        if h == i:
            continue
        slot = i if i < h else i - 1
        transfers.append(bass.RemoteDMATransfer(
            dst_ids=[dst_id(h)],
            dma_engine_mask=0b11 << (2 * len(transfers)),
            remote_sem=T.sem.arrived,
            src=T.xs[:, r * B:(r + 1) * B],
            dst=T.land[:, slot * B:(slot + 1) * B],
        ))
    g.remote_dma_fused(transfers, local_sem=T.sem.sent)

    g.wait_ge(T.sem.arrived, 2 * (N - 1))
    srcs = [T.land[:, s * B:(s + 1) * B] for s in range(N - 1)] + [T.xs[:, mine * B:(mine + 1) * B]]
    g.remote_dma_fused([bass.RemoteDMATransfer(
        dst_ids=[dst_id(mine)],
        dma_engine_mask=topo.mask(core, T.cores[mine]),
        remote_sem=T.sem.done,
        srcs=srcs,
        dsts=[T.res[:]],
        alu_op=2,
    )], local_sem=T.sem.sent)

    g.wait_ge(T.sem.done, 16)
    g.dma_start(T.y[:], T.res[:]).then_inc(T.sem.local, 16)
    g.wait_ge(T.sem.local, 32)
    g.wait_ge(T.sem.sent, 2 * (N - 1) + 16)
